import numpy as np
CORES = [2,10,50,58,66,74,122]
N = 7
T = 256
def entries(a): return a.T.reshape(-1)
def pack(v, P): return np.ascontiguousarray(np.asarray(v, np.int32).reshape(-1, P).T)
def lists(rng, how):
    n = rng.integers(0, T + 1, N)
    if how == "none": n[rng.integers(N)] = 0; n[0] = 0
    if how == "full": n[:] = T
    if how == "one": n[:] = 1
    if how == "lone": z = int(rng.integers(N)); n[:] = 0; n[z] = int(rng.integers(1, T + 1))
    if how == "void": n[:] = 0
    return {"ln": np.broadcast_to(pack(np.concatenate([n, np.zeros(32 - N, np.int64)]), 16), (N, 16, 2)).copy()}
def setup_inputs(rng):
    return dict({"x": rng.standard_normal((N, 128, T), dtype=np.float32)}, **lists(rng, "uniform"))
def setup_inputs_full(rng):
    d = setup_inputs(rng); d.update(lists(rng, "full"))
    for k in ("x",): d[k] = (d[k].astype(np.float32) * 1048576.0).astype(d[k].dtype)
    return d
def setup_inputs_lone(rng):
    d = setup_inputs(rng); d.update(lists(rng, "lone"))
    for k in ("x",): d[k] = (d[k].astype(np.float32) * (1 / 1024.0)).astype(d[k].dtype)
    return d
def setup_inputs_none(rng):
    d = setup_inputs(rng); d.update(lists(rng, "none"))
    return d
def setup_inputs_one(rng):
    d = setup_inputs(rng); d.update(lists(rng, "one"))
    return d
def setup_inputs_void(rng):
    d = setup_inputs(rng); d.update(lists(rng, "void"))
    return d
def check_inputs(x):
    bad = []
    if x["ln"].min() < 0 or x["ln"].max() >= T + 1: bad.append("ln out of range")
    if entries(x["ln"][0])[N:].any(): bad.append("an entry from N on isn't 0")
    if not all(np.array_equal(a, x["ln"][0]) for a in x["ln"]): bad.append("ln isn't alike on all ranks")
    return bad
def reference(x, ln):
    n = entries(ln[0]); got = np.concatenate([x[r][:, :n[r]] for r in range(N)], axis=1)
    y = np.zeros((128, N * T), x.dtype); y[:, :got.shape[1]] = got
    return {"y": np.broadcast_to(y, (N, 128, N * T))}

@@ -1,0 +1,191 @@
+from concourse.mybir import AluOpType
+
+N = 7
+W = 256
+Z = 16
+NC = N * W // 16
+JB = Z + W * (N - 1)
+U = 32
+
+DIRECT = [1, 2, 3, 5]
+HELP = [[4, 6]]
+ORDER = [1, 2, 3, 4, 5, 6]
+PMAX = 512
+
+SCRATCH = {
+    "win": ("sbuf", [128, Z + N * W], "float32"),
+    "ysb": ("sbuf", [128, N * W], "float32"),
+    "lnp": ("sbuf", [128, 2], "int32"),
+    "lnf": ("sbuf", [128, 1], "float32"),
+    "tri": ("sbuf", [128, 8], "float32"),
+    "rhs": ("sbuf", [128, 8], "float32"),
+    "ones": ("sbuf", [128, 128], "float32"),
+    "cps": ("psum", [128, 8], "float32"),
+    "c256": ("sbuf", [128, 8], "float32"),
+    "vi": ("sbuf", [128, NC], "int32"),
+    "va": ("sbuf", [128, NC], "int32"),
+    "vb": ("sbuf", [128, NC], "int32"),
+    "jj": ("sbuf", [128, NC], "float32"),
+    "thr": ("sbuf", [128, 8], "float32"),
+    "mul": ("sbuf", [128, 8], "float32"),
+    "tt": ("sbuf", [128, N * NC], "float32"),
+    "offf": ("sbuf", [128, NC], "float32"),
+    "off": ("sbuf", [128, NC], "uint16"),
+}
+SEMAPHORES = (["ld", "lnl", "msd", "gcd", "vsd", "rrd", "mmd", "sent", "std"]
+              + ["arr%d" % s for s in range(N)] + ["gp%d" % i for i in range(16)])
+
+
+def _bits(m):
+    return [b for b in range(32) if (m >> b) & 1]
+
+
+def _slot(s):
+    return Z + W * (N - 1 - s)
+
+
+def _helpers(topo, T, s):
+    me = T.cores[s]
+    same = [c for c in range(128) if topo.chip(c) == topo.chip(me) and c != me and T.rank_of(c) is None]
+    out = []
+    for i, ts in enumerate(HELP):
+        dsts = [T.cores[(s + t) % N] for t in ts]
+        want_other = (i % 2 == 0)
+        pick = [c for c in same if c not in out and all(topo.may_write(c, d) for d in dsts)
+                and ((topo.die(c) != topo.die(me)) == want_other)]
+        out.append(pick[0])
+    return out
+
+
+def _send(g, T, topo, src, dst, s, mask):
+    rid, pid, _ = topo.addr(dst)
+    ap = T.win[:, _slot(s):_slot(s) + W]
+    g.remote_dma(out_ap=ap, in_ap=ap, remote_sem=T.sem["arr%d" % s], local_sem=T.sem.sent,
+                 pid=pid, routing_id=rid, dma_engine_mask=mask)
+    return len(_bits(mask))
+
+
+def _pieces(d):
+    pos = {d: 0}
+    for i, t in enumerate(ORDER):
+        pos[(d - t) % N] = i + 1
+    rel = [max(pos[s] for s in range(k, N)) for k in range(N)]
+    groups = []
+    for k in range(N - 1, -1, -1):
+        if groups and groups[-1][2] == rel[k]:
+            groups[-1][0] = k
+        else:
+            groups.append([k, k + 1, rel[k]])
+    out = []
+    for k0, k1, _ in groups:
+        units = (k1 - k0) * W // U
+        n = -(-units * U // PMAX)
+        hi = k1 * W // U
+        for i in range(n):
+            u = units // n + (1 if i < units % n else 0)
+            out.append(((hi - u) * U, hi * U))
+            hi -= u
+    return out
+
+
+def _helper_program(g, core, T, topo):
+    for s in range(N):
+        hs = _helpers(topo, T, s)
+        if core not in hs:
+            continue
+        ts = HELP[hs.index(core)]
+        me = T.cores[s]
+        n_in = len(_bits(topo.mask(me, core) & ~topo.mask(me, T.cores[(s + 1) % N])))
+        g.wait_ge(T.sem["arr%d" % s], n_in)
+        tot = 0
+        for t in ts:
+            dst = T.cores[(s + t) % N]
+            tot += _send(g, T, topo, core, dst, s, topo.mask(core, dst))
+        g.wait_ge(T.sem.sent, tot)
+
+
+def rank_program(g, core, T, topo):
+    rank = T.rank_of(core)
+    if rank is None:
+        _helper_program(g, core, T, topo)
+        return
+    A = AluOpType
+    v = g.vector
+    sem = T.sem
+    own = T.win[:, _slot(rank):_slot(rank) + W]
+
+    g.sync.dma_start(own, T.x[:, :]).then_inc(sem.ld, 16)
+    g.scalar.dma_start(T.lnp[0:16, :], T.ln[:, :]).then_inc(sem.lnl, 16)
+
+    nv = [0]
+
+    def vdone(ins):
+        ins.then_inc(sem.vsd, 1)
+        nv[0] += 1
+
+    def vsync():
+        v.wait_ge(sem.vsd, nv[0])
+
+    v.memset(T.tri[0:16, 0:8], 1.0).then_inc(sem.msd, 1)
+    vdone(v.memset(T.ones[0:16, :], 1.0))
+    vdone(v.memset(T.win[:, 0:Z], 0.0))
+    g.iota(T.vi[:], [[128, NC]], 8 * JB, 1).then_inc(sem.gcd, 1)
+    g.iota(T.c256[:, 0:N], [[W, N]], W, 0, allow_small_or_imprecise_dtypes=True).then_inc(sem.gcd, 1)
+    g.wait_ge(sem.msd, 1)
+    g.affine_select(T.tri[0:16, 0:8], T.tri[0:16, 0:8], [[1, 8]], A.is_ge, 0.0, 0, -1).then_inc(sem.gcd, 1)
+
+    g.wait_ge(sem.ld, 16)
+    tot = 0
+    off_chip = topo.mask(core, T.cores[(rank + 1) % N])
+    for h in _helpers(topo, T, rank):
+        tot += _send(g, T, topo, core, h, rank, topo.mask(core, h) & ~off_chip)
+    for t in DIRECT:
+        dst = T.cores[(rank + t) % N]
+        tot += _send(g, T, topo, core, dst, rank, topo.mask(core, dst))
+
+    v.wait_ge(sem.gcd, 3)
+    vdone(v.tensor_scalar(T.va[:], T.vi[:], 15, None, A.bitwise_and))
+    vdone(v.tensor_scalar(T.vb[:], T.vi[:], 3, 0xFFF0, A.logical_shift_right, A.bitwise_and))
+    vsync()
+    vdone(v.tensor_tensor(T.jj[:], T.va[:], T.vb[:], A.add))
+    v.wait_ge(sem.lnl, 16)
+    vdone(v.tensor_copy(T.lnf[0:16, 0:1], T.lnp[0:16, 0:1]))
+    vsync()
+    v.tensor_scalar(T.rhs[0:16, 0:8], T.tri[0:16, 0:8], T.lnf[0:16, 0:1], None, A.mult).then_inc(sem.rrd, 1)
+    g.tensor.wait_ge(sem.rrd, 1)
+    g.tensor.matmul(T.cps[:, 0:8], T.ones[0:16, :], T.rhs[0:16, 0:8], True, True).then_inc(sem.mmd, 1)
+    v.wait_ge(sem.mmd, 1)
+    vdone(v.tensor_scalar(T.thr[:, 0:N], T.cps[:, 0:N], float(JB), None, A.add))
+    vdone(v.tensor_tensor(T.mul[:, 0:N], T.cps[:, 0:N], T.c256[:, 0:N], A.add))
+    vsync()
+    wid = [min(NC, 16 * (t + 2)) for t in range(N)]
+    for t in range(N):
+        m = T.mul[:, t:t + 1] if t < N - 1 else 100000.0
+        vdone(v.tensor_scalar(T.tt[:, NC * t:NC * t + wid[t]], T.jj[:, 0:wid[t]], T.thr[:, t:t + 1], m, A.is_ge, A.mult))
+    acc = NC * (N - 1)
+    for t in range(N - 2, -1, -1):
+        vsync()
+        vdone(v.tensor_tensor(T.tt[:, acc:acc + wid[t]], T.tt[:, acc:acc + wid[t]], T.tt[:, NC * t:NC * t + wid[t]], A.max))
+    vsync()
+    vdone(v.tensor_tensor(T.offf[:], T.jj[:], T.tt[:, acc:acc + NC], A.subtract))
+    vsync()
+    vdone(v.tensor_scalar(T.off[:], T.offf[:], 0.0, None, A.max))
+    vsync()
+
+    have = N
+    pieces = _pieces(rank)
+    for i, (j0, j1) in enumerate(pieces):
+        k0 = j0 // W
+        while have > k0:
+            have -= 1
+            if have == rank:
+                v.wait_ge(sem.ld, 16)
+            else:
+                v.wait_ge(sem["arr%d" % have], len(_bits(off_chip)))
+        v.tensor_copy(T.ysb[:, j0:j1], T.win[:, 0:Z + W * (N - k0)].indirect(T.off[:, j0 // 16:j1 // 16])).then_inc(sem["gp%d" % i], 1)
+        q = g.sync if i % 2 == 0 else g.scalar
+        q.wait_ge(sem["gp%d" % i], 1)
+        q.dma_start(T.y[:, j0:j1], T.ysb[:, j0:j1]).then_inc(sem.std, 16)
+
+    g.wait_ge(sem.sent, tot)
+    g.wait_ge(sem.std, 16 * len(pieces))

@@ -1,4 +1,4 @@
-from concourse.mybir import AluOpType
+from concourse.mybir import AluOpType, ActivationFunctionType
 
 N = 7
 W = 256
@@ -6,10 +6,14 @@ Z = 16
 NC = N * W // 16
 JB = Z + W * (N - 1)
 U = 32
+NM = 16 * N
+BIG = 4096
 
-DIRECT = [1, 2, 3, 5]
-HELP = [[4, 6]]
-ORDER = [1, 2, 3, 4, 5, 6]
+DIRECT = [1, 2, 3]
+HELP = [[4, 6], [5]]
+HELP_OTHER = [True, False]
+HAND_ALL = [False, False]
+ORDER = [[1], [2], [3], [5], [4], [6]]
 PMAX = 512
 
 SCRATCH = {
@@ -17,22 +21,20 @@ SCRATCH = {
     "ysb": ("sbuf", [128, N * W], "float32"),
     "lnp": ("sbuf", [128, 2], "int32"),
     "lnf": ("sbuf", [128, 1], "float32"),
-    "tri": ("sbuf", [128, 8], "float32"),
-    "rhs": ("sbuf", [128, 8], "float32"),
-    "ones": ("sbuf", [128, 128], "float32"),
-    "cps": ("psum", [128, 8], "float32"),
-    "c256": ("sbuf", [128, 8], "float32"),
-    "vi": ("sbuf", [128, NC], "int32"),
-    "va": ("sbuf", [128, NC], "int32"),
-    "vb": ("sbuf", [128, NC], "int32"),
-    "jj": ("sbuf", [128, NC], "float32"),
-    "thr": ("sbuf", [128, 8], "float32"),
-    "mul": ("sbuf", [128, 8], "float32"),
-    "tt": ("sbuf", [128, N * NC], "float32"),
-    "offf": ("sbuf", [128, NC], "float32"),
+    "lt": ("sbuf", [128, 128], "float32"),
+    "leq": ("sbuf", [128, NM], "float32"),
+    "cf": ("sbuf", [128, NC], "float32"),
+    "vi": ("sbuf", [128, 128], "int32"),
+    "va": ("sbuf", [128, 128], "int32"),
+    "pm": ("sbuf", [128, 128], "float32"),
+    "cc": ("sbuf", [128, 2], "float32"),
+    "tw": ("sbuf", [128, 2], "float32"),
+    "rr": ("sbuf", [128, NC], "float32"),
+    "cps": ("psum", [128, 512], "float32"),
+    "ops": ("psum", [128, 512], "float32"),
     "off": ("sbuf", [128, NC], "uint16"),
 }
-SEMAPHORES = (["ld", "lnl", "msd", "gcd", "vsd", "rrd", "mmd", "sent", "std"]
+SEMAPHORES = (["ld", "lnl", "msd", "gc1", "gc2", "gc3", "vsd", "rrd", "mmd", "sent", "std"]
               + ["arr%d" % s for s in range(N)] + ["gp%d" % i for i in range(16)])
 
 
@@ -50,11 +52,16 @@ def _helpers(topo, T, s):
     out = []
     for i, ts in enumerate(HELP):
         dsts = [T.cores[(s + t) % N] for t in ts]
-        want_other = (i % 2 == 0)
         pick = [c for c in same if c not in out and all(topo.may_write(c, d) for d in dsts)
-                and ((topo.die(c) != topo.die(me)) == want_other)]
+                and ((topo.die(c) != topo.die(me)) == HELP_OTHER[i])]
         out.append(pick[0])
     return out
+
+
+def _hand_mask(topo, T, s, i, h):
+    me = T.cores[s]
+    m = topo.mask(me, h)
+    return m if HAND_ALL[i] else m & ~topo.mask(me, T.cores[(s + 1) % N])
 
 
 def _send(g, T, topo, src, dst, s, mask):
@@ -67,8 +74,9 @@ def _send(g, T, topo, src, dst, s, mask):
 
 def _pieces(d):
     pos = {d: 0}
-    for i, t in enumerate(ORDER):
-        pos[(d - t) % N] = i + 1
+    for i, ts in enumerate(ORDER):
+        for t in ts:
+            pos[(d - t) % N] = i + 1
     rel = [max(pos[s] for s in range(k, N)) for k in range(N)]
     groups = []
     for k in range(N - 1, -1, -1):
@@ -93,12 +101,10 @@ def _helper_program(g, core, T, topo):
         hs = _helpers(topo, T, s)
         if core not in hs:
             continue
-        ts = HELP[hs.index(core)]
-        me = T.cores[s]
-        n_in = len(_bits(topo.mask(me, core) & ~topo.mask(me, T.cores[(s + 1) % N])))
-        g.wait_ge(T.sem["arr%d" % s], n_in)
+        i = hs.index(core)
+        g.wait_ge(T.sem["arr%d" % s], len(_bits(_hand_mask(topo, T, s, i, core))))
         tot = 0
-        for t in ts:
+        for t in HELP[i]:
             dst = T.cores[(s + t) % N]
             tot += _send(g, T, topo, core, dst, s, topo.mask(core, dst))
         g.wait_ge(T.sem.sent, tot)
@@ -126,64 +132,69 @@ def rank_program(g, core, T, topo):
     def vsync():
         v.wait_ge(sem.vsd, nv[0])
 
-    v.memset(T.tri[0:16, 0:8], 1.0).then_inc(sem.msd, 1)
-    vdone(v.memset(T.ones[0:16, :], 1.0))
+    v.memset(T.lt[0:16, :], 1.0).then_inc(sem.msd, 1)
     vdone(v.memset(T.win[:, 0:Z], 0.0))
-    g.iota(T.vi[:], [[128, NC]], 8 * JB, 1).then_inc(sem.gcd, 1)
-    g.iota(T.c256[:, 0:N], [[W, N]], W, 0, allow_small_or_imprecise_dtypes=True).then_inc(sem.gcd, 1)
+    vdone(v.memset(T.cc[0:96, 1:2], -float(W)))
+    vdone(v.memset(T.cc[96:128, 1:2], -float(BIG)))
+    g.iota(T.vi[:], [[-1, 128]], 128, 1).then_inc(sem.gc1, 1)
+    g.iota(T.cf[:], [[16, NC]], 0, 1, allow_small_or_imprecise_dtypes=True).then_inc(sem.gc2, 1)
     g.wait_ge(sem.msd, 1)
-    g.affine_select(T.tri[0:16, 0:8], T.tri[0:16, 0:8], [[1, 8]], A.is_ge, 0.0, 0, -1).then_inc(sem.gcd, 1)
+    g.affine_select(T.lt[0:16, :], T.lt[0:16, :], [[1, 128]], A.is_ge, 0.0, -16, -16).then_inc(sem.gc3, 1)
 
     g.wait_ge(sem.ld, 16)
     tot = 0
     off_chip = topo.mask(core, T.cores[(rank + 1) % N])
-    for h in _helpers(topo, T, rank):
-        tot += _send(g, T, topo, core, h, rank, topo.mask(core, h) & ~off_chip)
+    for i, h in enumerate(_helpers(topo, T, rank)):
+        tot += _send(g, T, topo, core, h, rank, _hand_mask(topo, T, rank, i, h))
     for t in DIRECT:
         dst = T.cores[(rank + t) % N]
         tot += _send(g, T, topo, core, dst, rank, topo.mask(core, dst))
 
-    v.wait_ge(sem.gcd, 3)
+    v.wait_ge(sem.gc1, 1)
     vdone(v.tensor_scalar(T.va[:], T.vi[:], 15, None, A.bitwise_and))
-    vdone(v.tensor_scalar(T.vb[:], T.vi[:], 3, 0xFFF0, A.logical_shift_right, A.bitwise_and))
     vsync()
-    vdone(v.tensor_tensor(T.jj[:], T.va[:], T.vb[:], A.add))
+    vdone(v.tensor_scalar(T.pm[:], T.va[:], 0, None, A.is_equal))
+    v.wait_ge(sem.gc2, 1)
+    vdone(v.tensor_tensor(T.cc[:, 0:1], T.cf[:, 0:1], T.va[:, 0:1], A.subtract))
+    vdone(v.tensor_scalar(T.rr[96:128, :], T.cf[96:128, :], float(JB - NM), None, A.add))
+    v.wait_ge(sem.gc3, 1)
+    vdone(v.tensor_tensor(T.leq[0:16, :], T.lt[0:16, 0:NM], T.lt[0:16, 16:16 + NM], A.subtract))
     v.wait_ge(sem.lnl, 16)
-    vdone(v.tensor_copy(T.lnf[0:16, 0:1], T.lnp[0:16, 0:1]))
     vsync()
-    v.tensor_scalar(T.rhs[0:16, 0:8], T.tri[0:16, 0:8], T.lnf[0:16, 0:1], None, A.mult).then_inc(sem.rrd, 1)
+    v.tensor_copy(T.lnf[0:16, 0:1], T.lnp[0:16, 0:1]).then_inc(sem.rrd, 1)
     g.tensor.wait_ge(sem.rrd, 1)
-    g.tensor.matmul(T.cps[:, 0:8], T.ones[0:16, :], T.rhs[0:16, 0:8], True, True).then_inc(sem.mmd, 1)
-    v.wait_ge(sem.mmd, 1)
-    vdone(v.tensor_scalar(T.thr[:, 0:N], T.cps[:, 0:N], float(JB), None, A.add))
-    vdone(v.tensor_tensor(T.mul[:, 0:N], T.cps[:, 0:N], T.c256[:, 0:N], A.add))
+    g.tensor.matmul(T.cps[0:NM, 0:1], T.lt[0:16, 16:16 + NM], T.lnf[0:16, 0:1], True, True).then_inc(sem.mmd, 1)
+    g.tensor.matmul(T.cps[0:NM, 1:2], T.leq[0:16, :], T.lnf[0:16, 0:1], True, True).then_inc(sem.mmd, 1)
+    v.wait_ge(sem.mmd, 2)
+    vdone(v.tensor_tensor(T.tw[0:NM, 0:2], T.cps[0:NM, 0:2], T.cc[0:NM, 0:2], A.add))
     vsync()
-    wid = [min(NC, 16 * (t + 2)) for t in range(N)]
-    for t in range(N):
-        m = T.mul[:, t:t + 1] if t < N - 1 else 100000.0
-        vdone(v.tensor_scalar(T.tt[:, NC * t:NC * t + wid[t]], T.jj[:, 0:wid[t]], T.thr[:, t:t + 1], m, A.is_ge, A.mult))
-    acc = NC * (N - 1)
-    for t in range(N - 2, -1, -1):
-        vsync()
-        vdone(v.tensor_tensor(T.tt[:, acc:acc + wid[t]], T.tt[:, acc:acc + wid[t]], T.tt[:, NC * t:NC * t + wid[t]], A.max))
+    v.tensor_scalar(T.rr[0:NM, :], T.cf[0:NM, :], T.tw[0:NM, 0:1], T.tw[0:NM, 1:2], A.is_ge, A.mult).then_inc(sem.rrd, 1)
+    g.tensor.wait_ge(sem.rrd, 2)
+    g.tensor.matmul(T.ops[:, 0:NC], T.pm[:], T.rr[:], True, True).then_inc(sem.mmd, 1)
+    v.wait_ge(sem.mmd, 3)
+    vdone(v.tensor_scalar(T.off[:], T.ops[:, 0:NC], 0.0, None, A.max))
     vsync()
-    vdone(v.tensor_tensor(T.offf[:], T.jj[:], T.tt[:, acc:acc + NC], A.subtract))
-    vsync()
-    vdone(v.tensor_scalar(T.off[:], T.offf[:], 0.0, None, A.max))
-    vsync()
+    g.scalar.wait_ge(sem.vsd, nv[0])
 
-    have = N
+    have = {0: N, 1: N}
     pieces = _pieces(rank)
     for i, (j0, j1) in enumerate(pieces):
         k0 = j0 // W
-        while have > k0:
-            have -= 1
-            if have == rank:
-                v.wait_ge(sem.ld, 16)
+        e = i % 2
+        cq = g.scalar if e else v
+        while have[e] > k0:
+            have[e] -= 1
+            if have[e] == rank:
+                cq.wait_ge(sem.ld, 16)
             else:
-                v.wait_ge(sem["arr%d" % have], len(_bits(off_chip)))
-        v.tensor_copy(T.ysb[:, j0:j1], T.win[:, 0:Z + W * (N - k0)].indirect(T.off[:, j0 // 16:j1 // 16])).then_inc(sem["gp%d" % i], 1)
-        q = g.sync if i % 2 == 0 else g.scalar
+                cq.wait_ge(sem["arr%d" % have[e]], len(_bits(off_chip)))
+        src = T.win[:, 0:Z + W * (N - k0)].indirect(T.off[:, j0 // 16:j1 // 16])
+        if e:
+            ins = g.scalar.activation(T.ysb[:, j0:j1], src, ActivationFunctionType.Identity, bias=-0.0)
+        else:
+            ins = v.tensor_copy(T.ysb[:, j0:j1], src)
+        ins.then_inc(sem["gp%d" % i], 1)
+        q = g.scalar if e else g.sync
         q.wait_ge(sem["gp%d" % i], 1)
         q.dma_start(T.y[:, j0:j1], T.ysb[:, j0:j1]).then_inc(sem.std, 16)
 

@@ -9,12 +9,13 @@ U = 32
 NM = 16 * N
 BIG = 4096
 
-DIRECT = [1, 2, 3]
-HELP = [[4, 6], [5]]
-HELP_OTHER = [True, False]
-HAND_ALL = [False, False]
-ORDER = [[1], [2], [3], [5], [4], [6]]
-PMAX = 512
+DIRECT = [1, 2]
+HELP = [[4, 6], [5], [3]]
+HELP_OTHER = [True, False, False]
+ORDER = [[1], [2], [4], [5], [6], [3]]
+RONE = 512
+RFIRST = 384
+RMAX = 768
 
 SCRATCH = {
     "win": ("sbuf", [128, Z + N * W], "float32"),
@@ -34,7 +35,7 @@ SCRATCH = {
     "ops": ("psum", [128, 512], "float32"),
     "off": ("sbuf", [128, NC], "uint16"),
 }
-SEMAPHORES = (["ld", "lnl", "msd", "gc1", "gc2", "gc3", "vsd", "rrd", "mmd", "sent", "std"]
+SEMAPHORES = (["ld", "lnl", "msd", "gtab", "tb0", "tb1", "tb2", "vsd", "rrd", "mmd", "sent", "std"]
               + ["arr%d" % s for s in range(N)] + ["gp%d" % i for i in range(16)])
 
 
@@ -52,19 +53,18 @@ def _helpers(topo, T, s):
     out = []
     for i, ts in enumerate(HELP):
         dsts = [T.cores[(s + t) % N] for t in ts]
-        pick = [c for c in same if c not in out and all(topo.may_write(c, d) for d in dsts)
-                and ((topo.die(c) != topo.die(me)) == HELP_OTHER[i])]
+        ok = [c for c in same if c not in out and all(topo.may_write(c, d) for d in dsts)]
+        pick = [c for c in ok if (topo.die(c) != topo.die(me)) == HELP_OTHER[i]] or ok
         out.append(pick[0])
     return out
 
 
-def _hand_mask(topo, T, s, i, h):
+def _hand_mask(topo, T, s, h):
     me = T.cores[s]
-    m = topo.mask(me, h)
-    return m if HAND_ALL[i] else m & ~topo.mask(me, T.cores[(s + 1) % N])
+    return topo.mask(me, h) & ~topo.mask(me, T.cores[(s + 1) % N])
 
 
-def _send(g, T, topo, src, dst, s, mask):
+def _send(g, T, topo, dst, s, mask):
     rid, pid, _ = topo.addr(dst)
     ap = T.win[:, _slot(s):_slot(s) + W]
     g.remote_dma(out_ap=ap, in_ap=ap, remote_sem=T.sem["arr%d" % s], local_sem=T.sem.sent,
@@ -72,7 +72,7 @@ def _send(g, T, topo, src, dst, s, mask):
     return len(_bits(mask))
 
 
-def _pieces(d):
+def _rounds(d):
     pos = {d: 0}
     for i, ts in enumerate(ORDER):
         for t in ts:
@@ -86,27 +86,50 @@ def _pieces(d):
             groups.append([k, k + 1, rel[k]])
     out = []
     for k0, k1, _ in groups:
-        units = (k1 - k0) * W // U
-        n = -(-units * U // PMAX)
-        hi = k1 * W // U
-        for i in range(n):
-            u = units // n + (1 if i < units % n else 0)
-            out.append(((hi - u) * U, hi * U))
-            hi -= u
+        n = (k1 - k0) * W
+        if n <= RONE:
+            sizes = [n]
+        else:
+            first = RFIRST if n > RMAX else RFIRST - 2 * U
+            units = (n - first) // (2 * U)
+            m = -(-(n - first) // RMAX)
+            sizes = [first] + [2 * U * (units // m + (1 if i < units % m else 0)) for i in range(m)]
+        hi = k1 * W
+        for sz in sizes:
+            out.append((hi - sz, hi - sz // 2, hi))
+            hi -= sz
     return out
 
 
 def _helper_program(g, core, T, topo):
+    A = AluOpType
     for s in range(N):
         hs = _helpers(topo, T, s)
         if core not in hs:
             continue
         i = hs.index(core)
-        g.wait_ge(T.sem["arr%d" % s], len(_bits(_hand_mask(topo, T, s, i, core))))
-        tot = 0
+        me = T.cores[s]
+        out_mask = topo.mask(core, T.cores[(s + HELP[i][0]) % N])
+        if i == 0:
+            tab = T.vi
+            g.iota(T.vi[:], [[-1, 128]], 128, 1).then_inc(T.sem.gtab, 1)
+        elif i == 1:
+            tab = T.cf
+            g.iota(T.cf[:], [[16, NC]], 0, 1, allow_small_or_imprecise_dtypes=True).then_inc(T.sem.gtab, 1)
+        else:
+            tab = T.lt
+            g.vector.memset(T.lt[:], 1.0).then_inc(T.sem.msd, 1)
+            g.wait_ge(T.sem.msd, 1)
+            g.affine_select(T.lt[0:16, :], T.lt[0:16, :], [[1, 128]], A.is_ge, 0.0, -16, -16).then_inc(T.sem.gtab, 1)
+        g.wait_ge(T.sem.gtab, 1)
+        rid, pid, _ = topo.addr(me)
+        g.remote_dma(out_ap=tab[:], in_ap=tab[:], remote_sem=T.sem["tb%d" % i], local_sem=T.sem.sent,
+                     pid=pid, routing_id=rid, dma_engine_mask=out_mask)
+        tot = len(_bits(out_mask))
+        g.wait_ge(T.sem["arr%d" % s], len(_bits(_hand_mask(topo, T, s, core))))
         for t in HELP[i]:
             dst = T.cores[(s + t) % N]
-            tot += _send(g, T, topo, core, dst, s, topo.mask(core, dst))
+            tot += _send(g, T, topo, dst, s, topo.mask(core, dst))
         g.wait_ge(T.sem.sent, tot)
 
 
@@ -119,6 +142,8 @@ def rank_program(g, core, T, topo):
     v = g.vector
     sem = T.sem
     own = T.win[:, _slot(rank):_slot(rank) + W]
+    hs = _helpers(topo, T, rank)
+    tbn = [len(_bits(topo.mask(h, T.cores[(rank + HELP[i][0]) % N]))) for i, h in enumerate(hs)]
 
     g.sync.dma_start(own, T.x[:, :]).then_inc(sem.ld, 16)
     g.scalar.dma_start(T.lnp[0:16, :], T.ln[:, :]).then_inc(sem.lnl, 16)
@@ -132,32 +157,27 @@ def rank_program(g, core, T, topo):
     def vsync():
         v.wait_ge(sem.vsd, nv[0])
 
-    v.memset(T.lt[0:16, :], 1.0).then_inc(sem.msd, 1)
     vdone(v.memset(T.win[:, 0:Z], 0.0))
     vdone(v.memset(T.cc[0:96, 1:2], -float(W)))
     vdone(v.memset(T.cc[96:128, 1:2], -float(BIG)))
-    g.iota(T.vi[:], [[-1, 128]], 128, 1).then_inc(sem.gc1, 1)
-    g.iota(T.cf[:], [[16, NC]], 0, 1, allow_small_or_imprecise_dtypes=True).then_inc(sem.gc2, 1)
-    g.wait_ge(sem.msd, 1)
-    g.affine_select(T.lt[0:16, :], T.lt[0:16, :], [[1, 128]], A.is_ge, 0.0, -16, -16).then_inc(sem.gc3, 1)
 
     g.wait_ge(sem.ld, 16)
     tot = 0
     off_chip = topo.mask(core, T.cores[(rank + 1) % N])
-    for i, h in enumerate(_helpers(topo, T, rank)):
-        tot += _send(g, T, topo, core, h, rank, _hand_mask(topo, T, rank, i, h))
-    for t in DIRECT:
-        dst = T.cores[(rank + t) % N]
-        tot += _send(g, T, topo, core, dst, rank, topo.mask(core, dst))
+    for i, h in enumerate(hs):
+        tot += _send(g, T, topo, h, rank, _hand_mask(topo, T, rank, h))
+        if i < len(DIRECT):
+            dst = T.cores[(rank + DIRECT[i]) % N]
+            tot += _send(g, T, topo, dst, rank, topo.mask(core, dst))
 
-    v.wait_ge(sem.gc1, 1)
+    v.wait_ge(sem.tb0, tbn[0])
     vdone(v.tensor_scalar(T.va[:], T.vi[:], 15, None, A.bitwise_and))
     vsync()
     vdone(v.tensor_scalar(T.pm[:], T.va[:], 0, None, A.is_equal))
-    v.wait_ge(sem.gc2, 1)
+    v.wait_ge(sem.tb1, tbn[1])
     vdone(v.tensor_tensor(T.cc[:, 0:1], T.cf[:, 0:1], T.va[:, 0:1], A.subtract))
     vdone(v.tensor_scalar(T.rr[96:128, :], T.cf[96:128, :], float(JB - NM), None, A.add))
-    v.wait_ge(sem.gc3, 1)
+    v.wait_ge(sem.tb2, tbn[2])
     vdone(v.tensor_tensor(T.leq[0:16, :], T.lt[0:16, 0:NM], T.lt[0:16, 16:16 + NM], A.subtract))
     v.wait_ge(sem.lnl, 16)
     vsync()
@@ -177,26 +197,25 @@ def rank_program(g, core, T, topo):
     g.scalar.wait_ge(sem.vsd, nv[0])
 
     have = {0: N, 1: N}
-    pieces = _pieces(rank)
-    for i, (j0, j1) in enumerate(pieces):
-        k0 = j0 // W
-        e = i % 2
-        cq = g.scalar if e else v
-        while have[e] > k0:
-            have[e] -= 1
-            if have[e] == rank:
-                cq.wait_ge(sem.ld, 16)
+    rounds = _rounds(rank)
+    for i, (j0, jm, j1) in enumerate(rounds):
+        for e, (a, b) in enumerate(((jm, j1), (j0, jm))):
+            k0 = a // W
+            cq = g.scalar if e else v
+            while have[e] > k0:
+                have[e] -= 1
+                if have[e] == rank:
+                    cq.wait_ge(sem.ld, 16)
+                else:
+                    cq.wait_ge(sem["arr%d" % have[e]], len(_bits(off_chip)))
+            src = T.win[:, 0:Z + W * (N - k0)].indirect(T.off[:, a // 16:b // 16])
+            if e:
+                ins = g.scalar.activation(T.ysb[:, a:b], src, ActivationFunctionType.Identity, bias=-0.0)
             else:
-                cq.wait_ge(sem["arr%d" % have[e]], len(_bits(off_chip)))
-        src = T.win[:, 0:Z + W * (N - k0)].indirect(T.off[:, j0 // 16:j1 // 16])
-        if e:
-            ins = g.scalar.activation(T.ysb[:, j0:j1], src, ActivationFunctionType.Identity, bias=-0.0)
-        else:
-            ins = v.tensor_copy(T.ysb[:, j0:j1], src)
-        ins.then_inc(sem["gp%d" % i], 1)
-        q = g.scalar if e else g.sync
-        q.wait_ge(sem["gp%d" % i], 1)
-        q.dma_start(T.y[:, j0:j1], T.ysb[:, j0:j1]).then_inc(sem.std, 16)
+                ins = v.tensor_copy(T.ysb[:, a:b], src)
+            ins.then_inc(sem["gp%d" % i], 1)
+        g.sync.wait_ge(sem["gp%d" % i], 2)
+        g.sync.dma_start(T.y[:, j0:j1], T.ysb[:, j0:j1]).then_inc(sem.std, 16)
 
     g.wait_ge(sem.sent, tot)
-    g.wait_ge(sem.std, 16 * len(pieces))
+    g.wait_ge(sem.std, 16 * len(rounds))

@@ -34,8 +34,9 @@ SCRATCH = {
     "cps": ("psum", [128, 512], "float32"),
     "ops": ("psum", [128, 512], "float32"),
     "off": ("sbuf", [128, NC], "uint16"),
+    "zs": ("sbuf", [128, Z], "float32"),
 }
-SEMAPHORES = (["ld", "lnl", "msd", "gtab", "tb0", "tb1", "tb2", "vsd", "rrd", "mmd", "sent", "std"]
+SEMAPHORES = (["zsd", "zc", "ld", "lnl", "msd", "gtab", "tb0", "tb1", "tb2", "vsd", "rrd", "mmd", "sent", "std"]
               + ["arr%d" % s for s in range(N)] + ["gp%d" % i for i in range(16)])
 
 
@@ -157,13 +158,19 @@ def rank_program(g, core, T, topo):
     def vsync():
         v.wait_ge(sem.vsd, nv[0])
 
-    vdone(v.memset(T.win[:, 0:Z], 0.0))
+    v.memset(T.zs[:], 0.0).then_inc(sem.zsd, 1)
     vdone(v.memset(T.cc[0:96, 1:2], -float(W)))
     vdone(v.memset(T.cc[96:128, 1:2], -float(BIG)))
 
+    nxt, prv = T.cores[(rank + 1) % N], T.cores[(rank - 1) % N]
+    off_chip = topo.mask(core, nxt)
+    g.wait_ge(sem.zsd, 1)
+    rid, pid, _ = topo.addr(nxt)
+    g.remote_dma(out_ap=T.win[:, 0:Z], in_ap=T.zs[:], remote_sem=sem.zc, local_sem=sem.sent,
+                 pid=pid, routing_id=rid, dma_engine_mask=off_chip)
+    tot = len(_bits(off_chip))
+
     g.wait_ge(sem.ld, 16)
-    tot = 0
-    off_chip = topo.mask(core, T.cores[(rank + 1) % N])
     for i, h in enumerate(hs):
         tot += _send(g, T, topo, h, rank, _hand_mask(topo, T, rank, h))
         if i < len(DIRECT):
@@ -195,6 +202,8 @@ def rank_program(g, core, T, topo):
     vdone(v.tensor_scalar(T.off[:], T.ops[:, 0:NC], 0.0, None, A.max))
     vsync()
     g.scalar.wait_ge(sem.vsd, nv[0])
+    v.wait_ge(sem.zc, len(_bits(topo.mask(prv, core))))
+    g.scalar.wait_ge(sem.zc, len(_bits(topo.mask(prv, core))))
 
     have = {0: N, 1: N}
     rounds = _rounds(rank)

from concourse.mybir import AluOpType, ActivationFunctionType

N = 7
W = 256
Z = 16
NC = N * W // 16
JB = Z + W * (N - 1)
U = 32
NM = 16 * N
BIG = 4096

DIRECT = [1, 2]
HELP = [[4, 6], [5], [3]]
HELP_OTHER = [True, False, False]
ORDER = [[1], [2], [4], [5], [6], [3]]
RONE = 512
RFIRST = 384
RMAX = 768

SCRATCH = {
    "win": ("sbuf", [128, Z + N * W], "float32"),
    "ysb": ("sbuf", [128, N * W], "float32"),
    "lnp": ("sbuf", [128, 2], "int32"),
    "lnf": ("sbuf", [128, 1], "float32"),
    "lt": ("sbuf", [128, 128], "float32"),
    "leq": ("sbuf", [128, NM], "float32"),
    "cf": ("sbuf", [128, NC], "float32"),
    "vi": ("sbuf", [128, 128], "int32"),
    "va": ("sbuf", [128, 128], "int32"),
    "pm": ("sbuf", [128, 128], "float32"),
    "cc": ("sbuf", [128, 2], "float32"),
    "tw": ("sbuf", [128, 2], "float32"),
    "rr": ("sbuf", [128, NC], "float32"),
    "cps": ("psum", [128, 512], "float32"),
    "ops": ("psum", [128, 512], "float32"),
    "off": ("sbuf", [128, NC], "uint16"),
    "zs": ("sbuf", [128, Z], "float32"),
}
SEMAPHORES = (["zsd", "zc", "ld", "lnl", "msd", "gtab", "tb0", "tb1", "tb2", "vsd", "rrd", "mmd", "sent", "std"]
              + ["arr%d" % s for s in range(N)] + ["gp%d" % i for i in range(16)])


def _bits(m):
    return [b for b in range(32) if (m >> b) & 1]


def _slot(s):
    return Z + W * (N - 1 - s)


def _helpers(topo, T, s):
    me = T.cores[s]
    same = [c for c in range(128) if topo.chip(c) == topo.chip(me) and c != me and T.rank_of(c) is None]
    out = []
    for i, ts in enumerate(HELP):
        dsts = [T.cores[(s + t) % N] for t in ts]
        ok = [c for c in same if c not in out and all(topo.may_write(c, d) for d in dsts)]
        pick = [c for c in ok if (topo.die(c) != topo.die(me)) == HELP_OTHER[i]] or ok
        out.append(pick[0])
    return out


def _hand_mask(topo, T, s, h):
    me = T.cores[s]
    return topo.mask(me, h) & ~topo.mask(me, T.cores[(s + 1) % N])


def _send(g, T, topo, dst, s, mask):
    rid, pid, _ = topo.addr(dst)
    ap = T.win[:, _slot(s):_slot(s) + W]
    g.remote_dma(out_ap=ap, in_ap=ap, remote_sem=T.sem["arr%d" % s], local_sem=T.sem.sent,
                 pid=pid, routing_id=rid, dma_engine_mask=mask)
    return len(_bits(mask))


def _rounds(d):
    pos = {d: 0}
    for i, ts in enumerate(ORDER):
        for t in ts:
            pos[(d - t) % N] = i + 1
    rel = [max(pos[s] for s in range(k, N)) for k in range(N)]
    groups = []
    for k in range(N - 1, -1, -1):
        if groups and groups[-1][2] == rel[k]:
            groups[-1][0] = k
        else:
            groups.append([k, k + 1, rel[k]])
    out = []
    for k0, k1, _ in groups:
        n = (k1 - k0) * W
        if n <= RONE:
            sizes = [n]
        else:
            first = RFIRST if n > RMAX else RFIRST - 2 * U
            units = (n - first) // (2 * U)
            m = -(-(n - first) // RMAX)
            sizes = [first] + [2 * U * (units // m + (1 if i < units % m else 0)) for i in range(m)]
        hi = k1 * W
        for sz in sizes:
            out.append((hi - sz, hi - sz // 2, hi))
            hi -= sz
    return out


def _helper_program(g, core, T, topo):
    A = AluOpType
    for s in range(N):
        hs = _helpers(topo, T, s)
        if core not in hs:
            continue
        i = hs.index(core)
        me = T.cores[s]
        out_mask = topo.mask(core, T.cores[(s + HELP[i][0]) % N])
        if i == 0:
            tab = T.vi
            g.iota(T.vi[:], [[-1, 128]], 128, 1).then_inc(T.sem.gtab, 1)
        elif i == 1:
            tab = T.cf
            g.iota(T.cf[:], [[16, NC]], 0, 1, allow_small_or_imprecise_dtypes=True).then_inc(T.sem.gtab, 1)
        else:
            tab = T.lt
            g.vector.memset(T.lt[:], 1.0).then_inc(T.sem.msd, 1)
            g.wait_ge(T.sem.msd, 1)
            g.affine_select(T.lt[0:16, :], T.lt[0:16, :], [[1, 128]], A.is_ge, 0.0, -16, -16).then_inc(T.sem.gtab, 1)
        g.wait_ge(T.sem.gtab, 1)
        rid, pid, _ = topo.addr(me)
        g.remote_dma(out_ap=tab[:], in_ap=tab[:], remote_sem=T.sem["tb%d" % i], local_sem=T.sem.sent,
                     pid=pid, routing_id=rid, dma_engine_mask=out_mask)
        tot = len(_bits(out_mask))
        g.wait_ge(T.sem["arr%d" % s], len(_bits(_hand_mask(topo, T, s, core))))
        for t in HELP[i]:
            dst = T.cores[(s + t) % N]
            tot += _send(g, T, topo, dst, s, topo.mask(core, dst))
        g.wait_ge(T.sem.sent, tot)


def rank_program(g, core, T, topo):
    rank = T.rank_of(core)
    if rank is None:
        _helper_program(g, core, T, topo)
        return
    A = AluOpType
    v = g.vector
    sem = T.sem
    own = T.win[:, _slot(rank):_slot(rank) + W]
    hs = _helpers(topo, T, rank)
    tbn = [len(_bits(topo.mask(h, T.cores[(rank + HELP[i][0]) % N]))) for i, h in enumerate(hs)]

    g.sync.dma_start(own, T.x[:, :]).then_inc(sem.ld, 16)
    g.scalar.dma_start(T.lnp[0:16, :], T.ln[:, :]).then_inc(sem.lnl, 16)

    nv = [0]

    def vdone(ins):
        ins.then_inc(sem.vsd, 1)
        nv[0] += 1

    def vsync():
        v.wait_ge(sem.vsd, nv[0])

    v.memset(T.zs[:], 0.0).then_inc(sem.zsd, 1)
    vdone(v.memset(T.cc[0:96, 1:2], -float(W)))
    vdone(v.memset(T.cc[96:128, 1:2], -float(BIG)))

    nxt, prv = T.cores[(rank + 1) % N], T.cores[(rank - 1) % N]
    off_chip = topo.mask(core, nxt)
    g.wait_ge(sem.zsd, 1)
    rid, pid, _ = topo.addr(nxt)
    g.remote_dma(out_ap=T.win[:, 0:Z], in_ap=T.zs[:], remote_sem=sem.zc, local_sem=sem.sent,
                 pid=pid, routing_id=rid, dma_engine_mask=off_chip)
    tot = len(_bits(off_chip))

    g.wait_ge(sem.ld, 16)
    for i, h in enumerate(hs):
        tot += _send(g, T, topo, h, rank, _hand_mask(topo, T, rank, h))
        if i < len(DIRECT):
            dst = T.cores[(rank + DIRECT[i]) % N]
            tot += _send(g, T, topo, dst, rank, topo.mask(core, dst))

    v.wait_ge(sem.tb0, tbn[0])
    vdone(v.tensor_scalar(T.va[:], T.vi[:], 15, None, A.bitwise_and))
    vsync()
    vdone(v.tensor_scalar(T.pm[:], T.va[:], 0, None, A.is_equal))
    v.wait_ge(sem.tb1, tbn[1])
    vdone(v.tensor_tensor(T.cc[:, 0:1], T.cf[:, 0:1], T.va[:, 0:1], A.subtract))
    vdone(v.tensor_scalar(T.rr[96:128, :], T.cf[96:128, :], float(JB - NM), None, A.add))
    v.wait_ge(sem.tb2, tbn[2])
    vdone(v.tensor_tensor(T.leq[0:16, :], T.lt[0:16, 0:NM], T.lt[0:16, 16:16 + NM], A.subtract))
    v.wait_ge(sem.lnl, 16)
    vsync()
    v.tensor_copy(T.lnf[0:16, 0:1], T.lnp[0:16, 0:1]).then_inc(sem.rrd, 1)
    g.tensor.wait_ge(sem.rrd, 1)
    g.tensor.matmul(T.cps[0:NM, 0:1], T.lt[0:16, 16:16 + NM], T.lnf[0:16, 0:1], True, True).then_inc(sem.mmd, 1)
    g.tensor.matmul(T.cps[0:NM, 1:2], T.leq[0:16, :], T.lnf[0:16, 0:1], True, True).then_inc(sem.mmd, 1)
    v.wait_ge(sem.mmd, 2)
    vdone(v.tensor_tensor(T.tw[0:NM, 0:2], T.cps[0:NM, 0:2], T.cc[0:NM, 0:2], A.add))
    vsync()
    v.tensor_scalar(T.rr[0:NM, :], T.cf[0:NM, :], T.tw[0:NM, 0:1], T.tw[0:NM, 1:2], A.is_ge, A.mult).then_inc(sem.rrd, 1)
    g.tensor.wait_ge(sem.rrd, 2)
    g.tensor.matmul(T.ops[:, 0:NC], T.pm[:], T.rr[:], True, True).then_inc(sem.mmd, 1)
    v.wait_ge(sem.mmd, 3)
    vdone(v.tensor_scalar(T.off[:], T.ops[:, 0:NC], 0.0, None, A.max))
    vsync()
    g.scalar.wait_ge(sem.vsd, nv[0])
    v.wait_ge(sem.zc, len(_bits(topo.mask(prv, core))))
    g.scalar.wait_ge(sem.zc, len(_bits(topo.mask(prv, core))))

    have = {0: N, 1: N}
    rounds = _rounds(rank)
    for i, (j0, jm, j1) in enumerate(rounds):
        for e, (a, b) in enumerate(((jm, j1), (j0, jm))):
            k0 = a // W
            cq = g.scalar if e else v
            while have[e] > k0:
                have[e] -= 1
                if have[e] == rank:
                    cq.wait_ge(sem.ld, 16)
                else:
                    cq.wait_ge(sem["arr%d" % have[e]], len(_bits(off_chip)))
            src = T.win[:, 0:Z + W * (N - k0)].indirect(T.off[:, a // 16:b // 16])
            if e:
                ins = g.scalar.activation(T.ysb[:, a:b], src, ActivationFunctionType.Identity, bias=-0.0)
            else:
                ins = v.tensor_copy(T.ysb[:, a:b], src)
            ins.then_inc(sem["gp%d" % i], 1)
        g.sync.wait_ge(sem["gp%d" % i], 2)
        g.sync.dma_start(T.y[:, j0:j1], T.ysb[:, j0:j1]).then_inc(sem.std, 16)

    g.wait_ge(sem.sent, tot)
    g.wait_ge(sem.std, 16 * len(rounds))
